import numpy as np
import ml_dtypes


def mxq(x, axis, fmt="e4m3"):
    dtype, down = {"e4m3": (ml_dtypes.float8_e4m3fn, 7), "e5m2": (ml_dtypes.float8_e5m2, 14)}[fmt]
    v = np.moveaxis(np.asarray(x, np.float32).astype(ml_dtypes.bfloat16).astype(np.float64), axis, -1)
    blocks = v.reshape(v.shape[:-1] + (-1, 32))
    amax = np.abs(blocks).max(-1, keepdims=True)
    byte = np.maximum(np.where(amax > 0, np.frexp(amax)[1] - 1 + 127, 0) - down, 1)
    scale = np.exp2(byte - 127.0)
    codes = (blocks / scale).astype(np.float32).astype(dtype).astype(np.float64)
    return np.moveaxis((codes * scale).reshape(v.shape), -1, axis)


WIDE = False


def mx_kscale(k):
    if not WIDE:
        return np.ones(k)
    levels = np.array([10, -10, 5, -5, 0])
    if k % 512:
        return np.exp2(np.random.permutation(np.resize(levels, k // 32))).repeat(32)
    a = np.empty((k // 512, 16))
    for p in range(k // 512):
        a[p, :8] = np.random.permutation(np.resize(levels, 8))
        for g in range(8):
            far = levels[np.abs(levels - a[p, g]) >= 10]
            a[p, g + 8] = far[np.random.randint(len(far))]
    return np.exp2(a.ravel()).repeat(32)


def f64(x):
    return np.asarray(x).astype(np.float64)


def striped(idx):
    return np.tile(idx.reshape(-1, 16).T, (8, 1)).astype(np.uint16)


def unstriped(offs):
    return offs[:16].T.reshape(-1).astype(np.int64)


def gelu(v):
    return 0.5 * v * (1.0 + np.tanh(np.sqrt(2.0 / np.pi) * (v + 0.044715 * v**3)))


K, T, D, V, H, N = 2048, 1024, 4, 512, 512, 512
P = 2 ** 7


def setup_inputs():
    n = np.random.standard_normal
    s = mx_kscale(K)[:, None]
    u = mx_kscale(H)
    return {
        "xT": (n((K, T)) * s).astype(np.float32),
        "w1": (n((K, H)) / np.sqrt(K) / s * u).astype(np.float32),
        "w2": (n((H, N)) / np.sqrt(H) / u[:, None]).astype(np.float32),
        "gate": np.tile(np.random.uniform(0.2, 1.0, (D, 1, V)) / np.sqrt(D), (1, P, 1)).astype(np.float32),
        "pos1": striped(np.random.permutation(T)[:V]),
        "pos2": striped(np.random.permutation(T)[:V]),
        "pos3": striped(np.random.permutation(T)[:V]),
        "pos4": striped(np.random.permutation(T)[:V]),
    }


def reference(xT, w1, w2, gate, pos1, pos2, pos3, pos4):
    h = gelu(mxq(f64(w1), 0, "e4m3").T @ mxq(f64(xT), 0, "e4m3"))
    z = sum(f64(gate)[d, :1] * h[:, unstriped(p)] for d, p in enumerate((pos1, pos2, pos3, pos4)))
    return mxq(f64(w2), 0, "e4m3").T @ mxq(z, 0, "e4m3")

@@ -1,0 +1,290 @@
+from contextlib import ExitStack
+
+import concourse.mybir as mybir
+from concourse.masks import make_identity
+
+K, T, D, V, H, N = 2048, 1024, 4, 512, 512, 512
+FLOPS = 2 * H * T * K + 2 * N * V * H
+
+F32 = mybir.dt.float32
+BF16 = mybir.dt.bfloat16
+U32 = mybir.dt.uint32
+U16 = mybir.dt.uint16
+U8 = mybir.dt.uint8
+FP8X4 = mybir.dt.float8_e4m3fn_x4
+ACT = mybir.ActivationFunctionType
+MULT = mybir.AluOpType.mult
+
+P = 128
+PACK = 4
+KP = K // (P * PACK)
+HALF = 512
+S_COLS = 192
+
+
+def tile_picked_gcn_mlp_gelu_sub_l_kernel(tc, xT, w1, w2, gate, pos1, pos2, pos3, pos4, out):
+    nc = tc.nc
+    with ExitStack() as ctx:
+        lists_pool = ctx.enter_context(tc.tile_pool(name="lists", bufs=1))
+        keep = ctx.enter_context(tc.tile_pool(name="keep", bufs=1))
+        stage = ctx.enter_context(tc.tile_pool(name="stage", bufs=3))
+        psum = ctx.enter_context(tc.psum_pool(name="psum", bufs=1))
+
+        offsets = []
+        for d in range(D):
+            off = lists_pool.tile([P, V // 16], U16, name=f"offsets{d}")
+            offsets.append(off)
+
+        ident32 = keep.tile([P, P], F32, name="ident32")
+        make_identity(nc, ident32[:])
+        ident16 = keep.tile([P, P], BF16, name="ident16")
+        make_identity(nc, ident16[:])
+        warm = keep.tile([P, 2], F32, name="warm")
+        nc.vector.memset(warm[:], 0.0)
+        nc.scalar.activation(warm[:, 1:2], warm[:, 0:1], ACT.Gelu_apprx_tanh)
+
+        w1_raw = {}
+        x_raw = {}
+
+        def load_w1(c, lo, width):
+            raw = keep.tile([P, PACK, width], F32, name=f"w1raw_{c}_{lo}", align_bytes=64)
+            rows = w1[c * 512 : (c + 1) * 512, lo : lo + width]
+            nc.sync.dma_start(out=raw[:], in_=rows.rearrange("(p j) i -> p j i", j=PACK))
+            for s in range(width // P):
+                w1_raw[(c, lo // P + s)] = (raw, s * P)
+
+        def load_x(c, lo, width):
+            raw = keep.tile([P, PACK, width], F32, name=f"xraw_{c}_{lo}", align_bytes=64)
+            rows = xT[c * 512 : (c + 1) * 512, lo : lo + width]
+            nc.sync.dma_start(out=raw[:], in_=rows.rearrange("(p j) t -> p j t", j=PACK))
+            x_raw[(c, lo)] = raw
+
+        X_CHUNKS = [[(0, 512), (512, 512)]] * (KP - 1) + [[(0, 512), (512, 256), (768, 256)]]
+        for c in range(KP):
+            load_w1(c, 0, P)
+            for lo, width in X_CHUNKS[c]:
+                load_x(c, lo, width)
+            if c == 1:
+                for d, pos in enumerate((pos1, pos2, pos3, pos4)):
+                    nc.sync.dma_start(offsets[d][:], pos)
+        gates = []
+        for d in range(D):
+            g = keep.tile([P, V], F32, name=f"gate{d}", align_bytes=64)
+            gates.append(g)
+        nc.sync.dma_start(out=gates[0][:], in_=gate[0])
+        for c in range(KP):
+            load_w1(c, P, P)
+        for d in range(1, D):
+            nc.sync.dma_start(out=gates[d][:], in_=gate[d])
+        for c in range(KP):
+            load_w1(c, 2 * P, 2 * P)
+        w2_raw = keep.tile([P, PACK, N], F32, name="w2raw", align_bytes=64)
+        nc.sync.dma_start(out=w2_raw[:], in_=w2.rearrange("(p j) m -> p j m", j=PACK))
+
+        x_codes = [keep.tile([P, T], U32, name=f"xcodes{c}", align_bytes=64) for c in range(KP)]
+        x_scales = [keep.tile([P, T], U8, name=f"xscales{c}", align_bytes=64) for c in range(KP)]
+        w1_codes = {}
+        w1_scales = {}
+        late_codes = {}
+        late_scales = {}
+        for m in (2, 3):
+            late_codes[m] = keep.tile([P, KP * P], U32, name=f"w1codes_{m}", align_bytes=64)
+            late_scales[m] = keep.tile([P, KP * P], U8, name=f"w1scales_{m}", align_bytes=64)
+            for c in range(KP):
+                w1_codes[(c, m)] = late_codes[m][:, c * P : (c + 1) * P]
+                w1_scales[(c, m)] = late_scales[m][:, c * P : (c + 1) * P]
+        for c in range(KP):
+            for m in range(2):
+                w1_codes[(c, m)] = keep.tile([P, P], U32, name=f"w1codes_{c}_{m}", align_bytes=64)[:]
+                w1_scales[(c, m)] = keep.tile([P, P], U8, name=f"w1scales_{c}_{m}", align_bytes=64)[:]
+        w2_codes = keep.tile([P, N], U32, name="w2codes", align_bytes=64)
+        w2_scales = keep.tile([P, N], U8, name="w2scales", align_bytes=64)
+        z_codes = keep.tile([P, V], U32, name="zcodes", align_bytes=64)
+        z_scales = keep.tile([P, V], U8, name="zscales", align_bytes=64)
+
+        def quantize(codes, scales, grouped):
+            nc.vector.quantize_mx(
+                out=codes.bitcast(FP8X4), scales=scales, in_=grouped[:].rearrange("p w j -> p (w j)")
+            )
+
+        def group_w1_vector(c, m):
+            raw, at = w1_raw[(c, m)]
+            grouped = stage.tile([P, P, PACK], BF16, name="wgrouped", tag="wgrouped", bufs=4, align_bytes=64)
+            nc.vector.tensor_copy(grouped[:], raw[:, :, at : at + P].rearrange("p j i -> p i j"))
+            return grouped
+
+        def group_w1(c, m):
+            raw, at = w1_raw[(c, m)]
+            grouped = stage.tile([P, P, PACK], BF16, name="wgrouped", tag="wgrouped", bufs=4, align_bytes=64)
+            nc.scalar.copy(grouped[:], raw[:, :, at : at + P].rearrange("p j i -> p i j"))
+            return grouped
+
+        def quant_w1(c, m, grouped):
+            quantize(w1_codes[(c, m)], w1_scales[(c, m)], grouped)
+
+        def prep_x(c, lo, width):
+            raw = x_raw[(c, lo)]
+            s = S_COLS * width // 512
+            grouped = stage.tile([P, width, PACK], BF16, name="xgrouped", tag="xgrouped", bufs=3, align_bytes=64)
+            nc.scalar.copy(grouped[:, 0:s, :], raw[:, :, 0:s].rearrange("p j t -> p t j"))
+            nc.vector.tensor_copy(grouped[:, s:width, :], raw[:, :, s:width].rearrange("p j t -> p t j"))
+            quantize(x_codes[c][:, lo : lo + width], x_scales[c][:, lo : lo + width], grouped)
+
+        def mm1(acc, c, m, n):
+            bank, lo, width = acc[n]
+            cols = slice(lo, lo + width)
+            nc.tensor.matmul_mx(
+                out=bank[:],
+                lhsT=w1_codes[(c, m)].bitcast(FP8X4),
+                lhsT_scale=w1_scales[(c, m)],
+                rhs=x_codes[c][:, cols].bitcast(FP8X4),
+                rhs_scale=x_scales[c][:, cols],
+                start=(c == 0),
+                stop=(c == KP - 1),
+            )
+
+        h = [keep.tile([P, T], F32, name=f"h{m}", align_bytes=64) for m in range(4)]
+
+        def new_acc(cuts):
+            acc = []
+            for tag, bufs, lo, width in cuts:
+                bank = psum.tile([P, width], F32, name=f"acc_{tag}", tag=tag, bufs=bufs)
+                acc.append((bank, lo, width))
+            return acc
+
+        def gelu(m, acc):
+            for bank, lo, width in acc:
+                nc.scalar.activation(h[m][:, lo : lo + width], bank[:], ACT.Gelu_apprx_tanh)
+
+        FIRST_CUTS = [("acc0", 1, 0, 512), ("acc1", 1, 512, 256), ("back", 2, 768, 256)]
+        CUTS = [("acc0", 1, 0, 512), ("acc1", 1, 512, 512)]
+
+        acc = new_acc(FIRST_CUTS)
+        for c in range(KP):
+            quant_w1(c, 0, group_w1(c, 0))
+            for lo, width in X_CHUNKS[c]:
+                prep_x(c, lo, width)
+            for n in range(3):
+                mm1(acc, c, 0, n)
+        gelu(0, acc)
+
+        zT = keep.tile([P, 4, PACK, P], BF16, name="zT", align_bytes=64)
+        zg = {}
+
+        def gather(m, d, v0, vn, parts):
+            part = stage.tile([P, vn], F32, name=f"part{d}", tag=f"part{d}", bufs=2, align_bytes=64)
+            nc.vector.tensor_tensor(
+                part[:], h[m][:].indirect(offsets[d][:, v0 // 16 : (v0 + vn) // 16]), gates[d][:, v0 : v0 + vn], MULT
+            )
+            parts.append(part)
+
+        def sums(d, part, v0, vn, banks):
+            for b in range(v0 // P, (v0 + vn) // P):
+                at = b * P - v0
+                nc.tensor.matmul(
+                    banks[b][:],
+                    lhsT=part[:, at : at + P],
+                    rhs=ident32[:],
+                    start=(d == 0),
+                    stop=(d == D - 1),
+                    is_transpose=True,
+                )
+
+        def put_zT(m, b, banks):
+            nc.scalar.copy(
+                zT[:, b, :, 32 * m : 32 * m + 32], banks[b][:].rearrange("v (q t) -> v t q", t=PACK)
+            )
+
+        def new_bank(b):
+            return psum.tile([P, P], F32, name=f"zs{b}", tag=f"zs{b}")
+
+        def group_late(m):
+            grouped = stage.tile([P, KP * P, PACK], BF16, name=f"wlate{m}", bufs=1, align_bytes=64)
+            for c in range(KP):
+                raw, at = w1_raw[(c, m)]
+                nc.scalar.copy(
+                    grouped[:, c * P : (c + 1) * P, :], raw[:, :, at : at + P].rearrange("p j i -> p i j")
+                )
+            return grouped
+
+        for c in (0, 1):
+            quant_w1(c, 1, group_w1_vector(c, 1))
+        for m in range(3):
+            nxt = new_acc(CUTS)
+            banks = {b: new_bank(b) for b in range(4)}
+            parts = []
+            for d in range(D):
+                gather(m, d, 0, V, parts)
+                if m == 0 and d == 0:
+                    for c in (2, 3):
+                        quant_w1(c, 1, group_w1(c, 1))
+                if m > 0 and d == 1:
+                    quantize(late_codes[m + 1][:], late_scales[m + 1][:], late)
+                if d == 1:
+                    for c in range(KP):
+                        for n in range(2):
+                            mm1(nxt, c, m + 1, n)
+                    gelu(m + 1, nxt)
+                sums(d, parts[d], 0, V, banks)
+                if d == 2 and m < 2:
+                    late = group_late(m + 2)
+            for b in range(4):
+                put_zT(m, b, banks)
+
+        w2_grouped = stage.tile([P, N, PACK], BF16, name="w2grouped", bufs=1, align_bytes=64)
+        for s in range(4):
+            nc.scalar.copy(
+                w2_grouped[:, s * P : (s + 1) * P, :], w2_raw[:, :, s * P : (s + 1) * P].rearrange("p j m -> p m j")
+            )
+
+        def turn_back(b, grouped, at, engine):
+            back = psum.tile([P, PACK, P], BF16, name="back", tag="back", bufs=2)
+            for t in range(PACK):
+                nc.tensor.transpose(back[:, t, :], zT[:, b, t, :], ident16[:])
+            view = back[:].rearrange("p t v -> p v t")
+            if engine == "s":
+                nc.scalar.copy(grouped[:, at : at + P, :], view)
+            else:
+                nc.vector.tensor_copy(grouped[:, at : at + P, :], view)
+
+        def second(grouped, v0, vn, tags):
+            cols = slice(v0, v0 + vn)
+            quantize(z_codes[:, cols], z_scales[:, cols], grouped)
+            for a in range(2):
+                o = psum.tile([P, 2, vn], F32, name="o", tag=tags[a])
+                for i in range(2):
+                    mt = 2 * a + i
+                    nc.tensor.matmul_mx(
+                        out=o[:, i, :],
+                        lhsT=w2_codes[:, mt * P : (mt + 1) * P].bitcast(FP8X4),
+                        lhsT_scale=w2_scales[:, mt * P : (mt + 1) * P],
+                        rhs=z_codes[:, cols].bitcast(FP8X4),
+                        rhs_scale=z_scales[:, cols],
+                        start=True,
+                        stop=True,
+                    )
+                res = stage.tile([P, 2, vn], F32, name="res", tag="res", bufs=6, align_bytes=64)
+                if a == 0:
+                    nc.vector.tensor_copy(res[:], o[:])
+                else:
+                    nc.scalar.copy(res[:], o[:])
+                nc.sync.dma_start(
+                    out=out[a * 256 : (a + 1) * 256, cols].rearrange("(i p) v -> p i v", p=P), in_=res[:]
+                )
+
+        CHUNKS = [(0, 256, ("acc0", "acc1")), (256, 128, ("zs0", "zs1")), (384, 128, ("acc0", "acc1"))]
+        for v0, vn, tags in CHUNKS:
+            grouped = keep.tile([P, vn, PACK], BF16, name=f"zg{v0}", align_bytes=64)
+            blocks = range(v0 // P, (v0 + vn) // P)
+            banks = {b: new_bank(b) for b in blocks}
+            parts = []
+            for d in range(D):
+                gather(3, d, v0, vn, parts)
+                sums(d, parts[d], v0, vn, banks)
+                if v0 == 0 and d == 1:
+                    quantize(w2_codes[:], w2_scales[:], w2_grouped)
+            for b in blocks:
+                put_zT(3, b, banks)
+            for b in blocks:
+                turn_back(b, grouped, b * P - v0, "v" if b == 3 else "s")
+            second(grouped, v0, vn, tags)

@@ -53,17 +53,19 @@ def tile_picked_gcn_mlp_gelu_sub_l_kernel(tc, xT, w1, w2, gate, pos1, pos2, pos3
             for s in range(width // P):
                 w1_raw[(c, lo // P + s)] = (raw, s * P)
 
-        def load_x(c, lo, width):
-            raw = keep.tile([P, PACK, width], F32, name=f"xraw_{c}_{lo}", align_bytes=64)
-            rows = xT[c * 512 : (c + 1) * 512, lo : lo + width]
-            nc.sync.dma_start(out=raw[:], in_=rows.rearrange("(p j) t -> p j t", j=PACK))
-            x_raw[(c, lo)] = raw
+        def load_x(c, pieces):
+            for lo, width in pieces:
+                raw = keep.tile([P, PACK, width], F32, name=f"xraw_{c}_{lo}", align_bytes=64)
+                rows = xT[c * 512 : (c + 1) * 512, lo : lo + width]
+                nc.sync.dma_start(out=raw[:], in_=rows.rearrange("(p j) t -> p j t", j=PACK))
+                for at in range(0, width, 256):
+                    x_raw[(c, lo + at)] = (raw, at)
 
+        LOADS = [[(0, T)]] * (KP - 1) + [[(0, 512), (512, 256), (768, 256)]]
         X_CHUNKS = [[(0, 512), (512, 512)]] * (KP - 1) + [[(0, 512), (512, 256), (768, 256)]]
         for c in range(KP):
             load_w1(c, 0, P)
-            for lo, width in X_CHUNKS[c]:
-                load_x(c, lo, width)
+            load_x(c, LOADS[c])
             if c == 1:
                 for d, pos in enumerate((pos1, pos2, pos3, pos4)):
                     nc.sync.dma_start(offsets[d][:], pos)
@@ -71,13 +73,21 @@ def tile_picked_gcn_mlp_gelu_sub_l_kernel(tc, xT, w1, w2, gate, pos1, pos2, pos3
         for d in range(D):
             g = keep.tile([P, V], F32, name=f"gate{d}", align_bytes=64)
             gates.append(g)
-        nc.sync.dma_start(out=gates[0][:], in_=gate[0])
-        for c in range(KP):
-            load_w1(c, P, P)
-        for d in range(1, D):
+
+        def load_gate(d):
             nc.sync.dma_start(out=gates[d][:], in_=gate[d])
-        for c in range(KP):
-            load_w1(c, 2 * P, 2 * P)
+
+        load_gate(0)
+        load_gate(1)
+        load_w1(0, P, P)
+        load_w1(1, P, P)
+        load_gate(2)
+        load_w1(2, P, P)
+        load_w1(3, P, P)
+        load_gate(3)
+        for m in (2, 3):
+            for c in range(KP):
+                load_w1(c, m * P, P)
         w2_raw = keep.tile([P, PACK, N], F32, name="w2raw", align_bytes=64)
         nc.sync.dma_start(out=w2_raw[:], in_=w2.rearrange("(p j) m -> p j m", j=PACK))
 
@@ -85,18 +95,16 @@ def tile_picked_gcn_mlp_gelu_sub_l_kernel(tc, xT, w1, w2, gate, pos1, pos2, pos3
         x_scales = [keep.tile([P, T], U8, name=f"xscales{c}", align_bytes=64) for c in range(KP)]
         w1_codes = {}
         w1_scales = {}
-        late_codes = {}
-        late_scales = {}
-        for m in (2, 3):
-            late_codes[m] = keep.tile([P, KP * P], U32, name=f"w1codes_{m}", align_bytes=64)
-            late_scales[m] = keep.tile([P, KP * P], U8, name=f"w1scales_{m}", align_bytes=64)
+        block_codes = []
+        block_scales = []
+        for m in range(4):
+            for_m = keep.tile([P, KP * P], U32, name=f"w1codes_{m}", align_bytes=64)
+            block_codes.append(for_m)
+            for_m = keep.tile([P, KP * P], U8, name=f"w1scales_{m}", align_bytes=64)
+            block_scales.append(for_m)
             for c in range(KP):
-                w1_codes[(c, m)] = late_codes[m][:, c * P : (c + 1) * P]
-                w1_scales[(c, m)] = late_scales[m][:, c * P : (c + 1) * P]
-        for c in range(KP):
-            for m in range(2):
-                w1_codes[(c, m)] = keep.tile([P, P], U32, name=f"w1codes_{c}_{m}", align_bytes=64)[:]
-                w1_scales[(c, m)] = keep.tile([P, P], U8, name=f"w1scales_{c}_{m}", align_bytes=64)[:]
+                w1_codes[(c, m)] = block_codes[m][:, c * P : (c + 1) * P]
+                w1_scales[(c, m)] = block_scales[m][:, c * P : (c + 1) * P]
         w2_codes = keep.tile([P, N], U32, name="w2codes", align_bytes=64)
         w2_scales = keep.tile([P, N], U8, name="w2scales", align_bytes=64)
         z_codes = keep.tile([P, V], U32, name="zcodes", align_bytes=64)
@@ -107,27 +115,23 @@ def tile_picked_gcn_mlp_gelu_sub_l_kernel(tc, xT, w1, w2, gate, pos1, pos2, pos3
                 out=codes.bitcast(FP8X4), scales=scales, in_=grouped[:].rearrange("p w j -> p (w j)")
             )
 
-        def group_w1_vector(c, m):
-            raw, at = w1_raw[(c, m)]
-            grouped = stage.tile([P, P, PACK], BF16, name="wgrouped", tag="wgrouped", bufs=4, align_bytes=64)
-            nc.vector.tensor_copy(grouped[:], raw[:, :, at : at + P].rearrange("p j i -> p i j"))
-            return grouped
-
-        def group_w1(c, m):
-            raw, at = w1_raw[(c, m)]
-            grouped = stage.tile([P, P, PACK], BF16, name="wgrouped", tag="wgrouped", bufs=4, align_bytes=64)
-            nc.scalar.copy(grouped[:], raw[:, :, at : at + P].rearrange("p j i -> p i j"))
-            return grouped
-
-        def quant_w1(c, m, grouped):
-            quantize(w1_codes[(c, m)], w1_scales[(c, m)], grouped)
+        def prep_w1(m, c0, n):
+            grouped = stage.tile([P, n * P, PACK], BF16, name="wgrouped", tag="wgrouped", bufs=4, align_bytes=64)
+            for c in range(c0, c0 + n):
+                raw, at = w1_raw[(c, m)]
+                nc.scalar.copy(
+                    grouped[:, (c - c0) * P : (c - c0 + 1) * P, :],
+                    raw[:, :, at : at + P].rearrange("p j i -> p i j"),
+                )
+            cols = slice(c0 * P, (c0 + n) * P)
+            quantize(block_codes[m][:, cols], block_scales[m][:, cols], grouped)
 
         def prep_x(c, lo, width):
-            raw = x_raw[(c, lo)]
+            raw, at = x_raw[(c, lo)]
             s = S_COLS * width // 512
             grouped = stage.tile([P, width, PACK], BF16, name="xgrouped", tag="xgrouped", bufs=3, align_bytes=64)
-            nc.scalar.copy(grouped[:, 0:s, :], raw[:, :, 0:s].rearrange("p j t -> p t j"))
-            nc.vector.tensor_copy(grouped[:, s:width, :], raw[:, :, s:width].rearrange("p j t -> p t j"))
+            nc.scalar.copy(grouped[:, 0:s, :], raw[:, :, at : at + s].rearrange("p j t -> p t j"))
+            nc.vector.tensor_copy(grouped[:, s:width, :], raw[:, :, at + s : at + width].rearrange("p j t -> p t j"))
             quantize(x_codes[c][:, lo : lo + width], x_scales[c][:, lo : lo + width], grouped)
 
         def mm1(acc, c, m, n):
@@ -161,7 +165,7 @@ def tile_picked_gcn_mlp_gelu_sub_l_kernel(tc, xT, w1, w2, gate, pos1, pos2, pos3
 
         acc = new_acc(FIRST_CUTS)
         for c in range(KP):
-            quant_w1(c, 0, group_w1(c, 0))
+            prep_w1(0, c, 1)
             for lo, width in X_CHUNKS[c]:
                 prep_x(c, lo, width)
             for n in range(3):
@@ -191,43 +195,30 @@ def tile_picked_gcn_mlp_gelu_sub_l_kernel(tc, xT, w1, w2, gate, pos1, pos2, pos3
                 )
 
         def put_zT(m, b, banks):
-            nc.scalar.copy(
-                zT[:, b, :, 32 * m : 32 * m + 32], banks[b][:].rearrange("v (q t) -> v t q", t=PACK)
-            )
+            to = zT[:, b, :, 32 * m : 32 * m + 32]
+            view = banks[b][:].rearrange("v (q t) -> v t q", t=PACK)
+            if m == 3 and b == 3:
+                nc.vector.tensor_copy(to, view)
+            else:
+                nc.scalar.copy(to, view)
 
         def new_bank(b):
             return psum.tile([P, P], F32, name=f"zs{b}", tag=f"zs{b}")
 
-        def group_late(m):
-            grouped = stage.tile([P, KP * P, PACK], BF16, name=f"wlate{m}", bufs=1, align_bytes=64)
-            for c in range(KP):
-                raw, at = w1_raw[(c, m)]
-                nc.scalar.copy(
-                    grouped[:, c * P : (c + 1) * P, :], raw[:, :, at : at + P].rearrange("p j i -> p i j")
-                )
-            return grouped
-
-        for c in (0, 1):
-            quant_w1(c, 1, group_w1_vector(c, 1))
         for m in range(3):
             nxt = new_acc(CUTS)
             banks = {b: new_bank(b) for b in range(4)}
             parts = []
             for d in range(D):
                 gather(m, d, 0, V, parts)
-                if m == 0 and d == 0:
-                    for c in (2, 3):
-                        quant_w1(c, 1, group_w1(c, 1))
-                if m > 0 and d == 1:
-                    quantize(late_codes[m + 1][:], late_scales[m + 1][:], late)
-                if d == 1:
-                    for c in range(KP):
+                if d < 2:
+                    prep_w1(m + 1, 2 * d, 2)
+                    for c in (2 * d, 2 * d + 1):
                         for n in range(2):
                             mm1(nxt, c, m + 1, n)
+                if d == 1:
                     gelu(m + 1, nxt)
                 sums(d, parts[d], 0, V, banks)
-                if d == 2 and m < 2:
-                    late = group_late(m + 2)
             for b in range(4):
                 put_zT(m, b, banks)
 
@@ -264,7 +255,7 @@ def tile_picked_gcn_mlp_gelu_sub_l_kernel(tc, xT, w1, w2, gate, pos1, pos2, pos3
                         stop=True,
                     )
                 res = stage.tile([P, 2, vn], F32, name="res", tag="res", bufs=6, align_bytes=64)
-                if a == 0:
+                if a == 0 and v0 == 384:
                     nc.vector.tensor_copy(res[:], o[:])
                 else:
                     nc.scalar.copy(res[:], o[:])

@@ -5,6 +5,7 @@ from concourse.masks import make_identity
 
 K, T, D, V, H, N = 2048, 1024, 4, 512, 512, 512
 FLOPS = 2 * H * T * K + 2 * N * V * H
+BYTES = 4 * (K * T + K * H + H * N + D * V + N * V) + 2 * D * 128 * (V // 16)
 
 F32 = mybir.dt.float32
 BF16 = mybir.dt.bfloat16
@@ -43,6 +44,9 @@ def tile_picked_gcn_mlp_gelu_sub_l_kernel(tc, xT, w1, w2, gate, pos1, pos2, pos3
         nc.vector.memset(warm[:], 0.0)
         nc.scalar.activation(warm[:, 1:2], warm[:, 0:1], ACT.Gelu_apprx_tanh)
 
+        gate_rows = keep.tile([P, V], F32, name="gate_rows", align_bytes=64)
+        nc.vector.memset(gate_rows[:], 0.0)
+
         w1_raw = {}
         x_raw = {}
 
@@ -69,23 +73,8 @@ def tile_picked_gcn_mlp_gelu_sub_l_kernel(tc, xT, w1, w2, gate, pos1, pos2, pos3
             if c == 1:
                 for d, pos in enumerate((pos1, pos2, pos3, pos4)):
                     nc.sync.dma_start(offsets[d][:], pos)
-        gates = []
-        for d in range(D):
-            g = keep.tile([P, V], F32, name=f"gate{d}", align_bytes=64)
-            gates.append(g)
-
-        def load_gate(d):
-            nc.sync.dma_start(out=gates[d][:], in_=gate[d])
-
-        load_gate(0)
-        load_gate(1)
-        load_w1(0, P, P)
-        load_w1(1, P, P)
-        load_gate(2)
-        load_w1(2, P, P)
-        load_w1(3, P, P)
-        load_gate(3)
-        for m in (2, 3):
+                nc.sync.dma_start(gate_rows[0:D, :], gate[:, 0, :])
+        for m in (1, 2, 3):
             for c in range(KP):
                 load_w1(c, m * P, P)
         w2_raw = keep.tile([P, PACK, N], F32, name="w2raw", align_bytes=64)
@@ -163,6 +152,24 @@ def tile_picked_gcn_mlp_gelu_sub_l_kernel(tc, xT, w1, w2, gate, pos1, pos2, pos3
         FIRST_CUTS = [("acc0", 1, 0, 512), ("acc1", 1, 512, 256), ("back", 2, 768, 256)]
         CUTS = [("acc0", 1, 0, 512), ("acc1", 1, 512, 512)]
 
+        gates = []
+
+        def spread_gates():
+            turned = psum.tile([P, 4, P], F32, name="turned", tag="zs0")
+            for b in range(4):
+                nc.tensor.transpose(turned[:, b, :], gate_rows[:, b * P : (b + 1) * P], ident32[:])
+            columns = keep.tile([P, 4, D], F32, name="gate_columns")
+            nc.vector.tensor_copy(columns[:], turned[:, :, 0:D])
+            for d in range(D):
+                bank = psum.tile([P, V], F32, name="gate_bank", tag=f"zs{(d + 1) % 4}")
+                for b in range(4):
+                    nc.tensor.transpose(
+                        bank[:, b * P : (b + 1) * P], columns[:, b, d : d + 1].to_broadcast([P, P]), ident32[:]
+                    )
+                g = keep.tile([P, V], F32, name=f"gate{d}", align_bytes=64)
+                nc.vector.tensor_copy(g[:], bank[:])
+                gates.append(g)
+
         acc = new_acc(FIRST_CUTS)
         for c in range(KP):
             prep_w1(0, c, 1)
@@ -170,6 +177,8 @@ def tile_picked_gcn_mlp_gelu_sub_l_kernel(tc, xT, w1, w2, gate, pos1, pos2, pos3
                 prep_x(c, lo, width)
             for n in range(3):
                 mm1(acc, c, 0, n)
+            if c == 1:
+                spread_gates()
         gelu(0, acc)
 
         zT = keep.tile([P, 4, PACK, P], BF16, name="zT", align_bytes=64)

@@ -99,6 +99,14 @@ def tile_picked_gcn_mlp_gelu_sub_l_kernel(tc, xT, w1, w2, gate, pos1, pos2, pos3
         z_codes = keep.tile([P, V], U32, name="zcodes", align_bytes=64)
         z_scales = keep.tile([P, V], U8, name="zscales", align_bytes=64)
 
+        def interleave(engine, to, rows):
+            to = to.rearrange("p (c i) j -> p c j i", i=4)
+            rows = rows.rearrange("p j (c i) -> p c j i", i=4)
+            if engine == "s":
+                nc.scalar.copy(to, rows)
+            else:
+                nc.vector.tensor_copy(to, rows)
+
         def quantize(codes, scales, grouped):
             nc.vector.quantize_mx(
                 out=codes.bitcast(FP8X4), scales=scales, in_=grouped[:].rearrange("p w j -> p (w j)")
@@ -108,10 +116,7 @@ def tile_picked_gcn_mlp_gelu_sub_l_kernel(tc, xT, w1, w2, gate, pos1, pos2, pos3
             grouped = stage.tile([P, n * P, PACK], BF16, name="wgrouped", tag="wgrouped", bufs=4, align_bytes=64)
             for c in range(c0, c0 + n):
                 raw, at = w1_raw[(c, m)]
-                nc.scalar.copy(
-                    grouped[:, (c - c0) * P : (c - c0 + 1) * P, :],
-                    raw[:, :, at : at + P].rearrange("p j i -> p i j"),
-                )
+                interleave("s", grouped[:, (c - c0) * P : (c - c0 + 1) * P, :], raw[:, :, at : at + P])
             cols = slice(c0 * P, (c0 + n) * P)
             quantize(block_codes[m][:, cols], block_scales[m][:, cols], grouped)
 
@@ -119,8 +124,8 @@ def tile_picked_gcn_mlp_gelu_sub_l_kernel(tc, xT, w1, w2, gate, pos1, pos2, pos3
             raw, at = x_raw[(c, lo)]
             s = S_COLS * width // 512
             grouped = stage.tile([P, width, PACK], BF16, name="xgrouped", tag="xgrouped", bufs=3, align_bytes=64)
-            nc.scalar.copy(grouped[:, 0:s, :], raw[:, :, at : at + s].rearrange("p j t -> p t j"))
-            nc.vector.tensor_copy(grouped[:, s:width, :], raw[:, :, at + s : at + width].rearrange("p j t -> p t j"))
+            interleave("s", grouped[:, 0:s, :], raw[:, :, at : at + s])
+            interleave("v", grouped[:, s:width, :], raw[:, :, at + s : at + width])
             quantize(x_codes[c][:, lo : lo + width], x_scales[c][:, lo : lo + width], grouped)
 
         def mm1(acc, c, m, n):
@@ -232,10 +237,8 @@ def tile_picked_gcn_mlp_gelu_sub_l_kernel(tc, xT, w1, w2, gate, pos1, pos2, pos3
                 put_zT(m, b, banks)
 
         w2_grouped = stage.tile([P, N, PACK], BF16, name="w2grouped", bufs=1, align_bytes=64)
-        for s in range(4):
-            nc.scalar.copy(
-                w2_grouped[:, s * P : (s + 1) * P, :], w2_raw[:, :, s * P : (s + 1) * P].rearrange("p j m -> p m j")
-            )
+        for s in range(2):
+            interleave("s", w2_grouped[:, s * 256 : (s + 1) * 256, :], w2_raw[:, :, s * 256 : (s + 1) * 256])
 
         def turn_back(b, grouped, at, engine):
             back = psum.tile([P, PACK, P], BF16, name="back", tag="back", bufs=2)

from contextlib import ExitStack

import concourse.mybir as mybir
from concourse.masks import make_identity

K, T, D, V, H, N = 2048, 1024, 4, 512, 512, 512
FLOPS = 2 * H * T * K + 2 * N * V * H
BYTES = 4 * (K * T + K * H + H * N + D * V + N * V) + 2 * D * 128 * (V // 16)

F32 = mybir.dt.float32
BF16 = mybir.dt.bfloat16
U32 = mybir.dt.uint32
U16 = mybir.dt.uint16
U8 = mybir.dt.uint8
FP8X4 = mybir.dt.float8_e4m3fn_x4
ACT = mybir.ActivationFunctionType
MULT = mybir.AluOpType.mult

P = 128
PACK = 4
KP = K // (P * PACK)
HALF = 512
S_COLS = 192


def tile_picked_gcn_mlp_gelu_sub_l_kernel(tc, xT, w1, w2, gate, pos1, pos2, pos3, pos4, out):
    nc = tc.nc
    with ExitStack() as ctx:
        lists_pool = ctx.enter_context(tc.tile_pool(name="lists", bufs=1))
        keep = ctx.enter_context(tc.tile_pool(name="keep", bufs=1))
        stage = ctx.enter_context(tc.tile_pool(name="stage", bufs=3))
        psum = ctx.enter_context(tc.psum_pool(name="psum", bufs=1))

        offsets = []
        for d in range(D):
            off = lists_pool.tile([P, V // 16], U16, name=f"offsets{d}")
            offsets.append(off)

        ident32 = keep.tile([P, P], F32, name="ident32")
        make_identity(nc, ident32[:])
        ident16 = keep.tile([P, P], BF16, name="ident16")
        make_identity(nc, ident16[:])
        warm = keep.tile([P, 2], F32, name="warm")
        nc.vector.memset(warm[:], 0.0)
        nc.scalar.activation(warm[:, 1:2], warm[:, 0:1], ACT.Gelu_apprx_tanh)

        gate_rows = keep.tile([P, V], F32, name="gate_rows", align_bytes=64)
        nc.vector.memset(gate_rows[:], 0.0)

        w1_raw = {}
        x_raw = {}

        def load_w1(c, lo, width):
            raw = keep.tile([P, PACK, width], F32, name=f"w1raw_{c}_{lo}", align_bytes=64)
            rows = w1[c * 512 : (c + 1) * 512, lo : lo + width]
            nc.sync.dma_start(out=raw[:], in_=rows.rearrange("(p j) i -> p j i", j=PACK))
            for s in range(width // P):
                w1_raw[(c, lo // P + s)] = (raw, s * P)

        def load_x(c, pieces):
            for lo, width in pieces:
                raw = keep.tile([P, PACK, width], F32, name=f"xraw_{c}_{lo}", align_bytes=64)
                rows = xT[c * 512 : (c + 1) * 512, lo : lo + width]
                nc.sync.dma_start(out=raw[:], in_=rows.rearrange("(p j) t -> p j t", j=PACK))
                for at in range(0, width, 256):
                    x_raw[(c, lo + at)] = (raw, at)

        LOADS = [[(0, T)]] * (KP - 1) + [[(0, 512), (512, 256), (768, 256)]]
        X_CHUNKS = [[(0, 512), (512, 512)]] * (KP - 1) + [[(0, 512), (512, 256), (768, 256)]]
        for c in range(KP):
            load_w1(c, 0, P)
            load_x(c, LOADS[c])
            if c == 1:
                for d, pos in enumerate((pos1, pos2, pos3, pos4)):
                    nc.sync.dma_start(offsets[d][:], pos)
                nc.sync.dma_start(gate_rows[0:D, :], gate[:, 0, :])
        for m in (1, 2, 3):
            for c in range(KP):
                load_w1(c, m * P, P)
        w2_raw = keep.tile([P, PACK, N], F32, name="w2raw", align_bytes=64)
        nc.sync.dma_start(out=w2_raw[:], in_=w2.rearrange("(p j) m -> p j m", j=PACK))

        x_codes = [keep.tile([P, T], U32, name=f"xcodes{c}", align_bytes=64) for c in range(KP)]
        x_scales = [keep.tile([P, T], U8, name=f"xscales{c}", align_bytes=64) for c in range(KP)]
        w1_codes = {}
        w1_scales = {}
        block_codes = []
        block_scales = []
        for m in range(4):
            for_m = keep.tile([P, KP * P], U32, name=f"w1codes_{m}", align_bytes=64)
            block_codes.append(for_m)
            for_m = keep.tile([P, KP * P], U8, name=f"w1scales_{m}", align_bytes=64)
            block_scales.append(for_m)
            for c in range(KP):
                w1_codes[(c, m)] = block_codes[m][:, c * P : (c + 1) * P]
                w1_scales[(c, m)] = block_scales[m][:, c * P : (c + 1) * P]
        w2_codes = keep.tile([P, N], U32, name="w2codes", align_bytes=64)
        w2_scales = keep.tile([P, N], U8, name="w2scales", align_bytes=64)
        z_codes = keep.tile([P, V], U32, name="zcodes", align_bytes=64)
        z_scales = keep.tile([P, V], U8, name="zscales", align_bytes=64)

        def interleave(engine, to, rows):
            to = to.rearrange("p (c i) j -> p c j i", i=4)
            rows = rows.rearrange("p j (c i) -> p c j i", i=4)
            if engine == "s":
                nc.scalar.copy(to, rows)
            else:
                nc.vector.tensor_copy(to, rows)

        def quantize(codes, scales, grouped):
            nc.vector.quantize_mx(
                out=codes.bitcast(FP8X4), scales=scales, in_=grouped[:].rearrange("p w j -> p (w j)")
            )

        def prep_w1(m, c0, n):
            grouped = stage.tile([P, n * P, PACK], BF16, name="wgrouped", tag="wgrouped", bufs=4, align_bytes=64)
            for c in range(c0, c0 + n):
                raw, at = w1_raw[(c, m)]
                interleave("s", grouped[:, (c - c0) * P : (c - c0 + 1) * P, :], raw[:, :, at : at + P])
            cols = slice(c0 * P, (c0 + n) * P)
            quantize(block_codes[m][:, cols], block_scales[m][:, cols], grouped)

        def prep_x(c, lo, width):
            raw, at = x_raw[(c, lo)]
            s = S_COLS * width // 512
            grouped = stage.tile([P, width, PACK], BF16, name="xgrouped", tag="xgrouped", bufs=3, align_bytes=64)
            interleave("s", grouped[:, 0:s, :], raw[:, :, at : at + s])
            interleave("v", grouped[:, s:width, :], raw[:, :, at + s : at + width])
            quantize(x_codes[c][:, lo : lo + width], x_scales[c][:, lo : lo + width], grouped)

        def mm1(acc, c, m, n):
            bank, lo, width = acc[n]
            cols = slice(lo, lo + width)
            nc.tensor.matmul_mx(
                out=bank[:],
                lhsT=w1_codes[(c, m)].bitcast(FP8X4),
                lhsT_scale=w1_scales[(c, m)],
                rhs=x_codes[c][:, cols].bitcast(FP8X4),
                rhs_scale=x_scales[c][:, cols],
                start=(c == 0),
                stop=(c == KP - 1),
            )

        h = [keep.tile([P, T], F32, name=f"h{m}", align_bytes=64) for m in range(4)]

        def new_acc(cuts):
            acc = []
            for tag, bufs, lo, width in cuts:
                bank = psum.tile([P, width], F32, name=f"acc_{tag}", tag=tag, bufs=bufs)
                acc.append((bank, lo, width))
            return acc

        def gelu(m, acc):
            for bank, lo, width in acc:
                nc.scalar.activation(h[m][:, lo : lo + width], bank[:], ACT.Gelu_apprx_tanh)

        FIRST_CUTS = [("acc0", 1, 0, 512), ("acc1", 1, 512, 256), ("back", 2, 768, 256)]
        CUTS = [("acc0", 1, 0, 512), ("acc1", 1, 512, 512)]

        gates = []

        def spread_gates():
            turned = psum.tile([P, 4, P], F32, name="turned", tag="zs0")
            for b in range(4):
                nc.tensor.transpose(turned[:, b, :], gate_rows[:, b * P : (b + 1) * P], ident32[:])
            columns = keep.tile([P, 4, D], F32, name="gate_columns")
            nc.vector.tensor_copy(columns[:], turned[:, :, 0:D])
            for d in range(D):
                bank = psum.tile([P, V], F32, name="gate_bank", tag=f"zs{(d + 1) % 4}")
                for b in range(4):
                    nc.tensor.transpose(
                        bank[:, b * P : (b + 1) * P], columns[:, b, d : d + 1].to_broadcast([P, P]), ident32[:]
                    )
                g = keep.tile([P, V], F32, name=f"gate{d}", align_bytes=64)
                nc.vector.tensor_copy(g[:], bank[:])
                gates.append(g)

        acc = new_acc(FIRST_CUTS)
        for c in range(KP):
            prep_w1(0, c, 1)
            for lo, width in X_CHUNKS[c]:
                prep_x(c, lo, width)
            for n in range(3):
                mm1(acc, c, 0, n)
            if c == 1:
                spread_gates()
        gelu(0, acc)

        zT = keep.tile([P, 4, PACK, P], BF16, name="zT", align_bytes=64)
        zg = {}

        def gather(m, d, v0, vn, parts):
            part = stage.tile([P, vn], F32, name=f"part{d}", tag=f"part{d}", bufs=2, align_bytes=64)
            nc.vector.tensor_tensor(
                part[:], h[m][:].indirect(offsets[d][:, v0 // 16 : (v0 + vn) // 16]), gates[d][:, v0 : v0 + vn], MULT
            )
            parts.append(part)

        def sums(d, part, v0, vn, banks):
            for b in range(v0 // P, (v0 + vn) // P):
                at = b * P - v0
                nc.tensor.matmul(
                    banks[b][:],
                    lhsT=part[:, at : at + P],
                    rhs=ident32[:],
                    start=(d == 0),
                    stop=(d == D - 1),
                    is_transpose=True,
                )

        def put_zT(m, b, banks):
            to = zT[:, b, :, 32 * m : 32 * m + 32]
            view = banks[b][:].rearrange("v (q t) -> v t q", t=PACK)
            if m == 3 and b == 3:
                nc.vector.tensor_copy(to, view)
            else:
                nc.scalar.copy(to, view)

        def new_bank(b):
            return psum.tile([P, P], F32, name=f"zs{b}", tag=f"zs{b}")

        for m in range(3):
            nxt = new_acc(CUTS)
            banks = {b: new_bank(b) for b in range(4)}
            parts = []
            for d in range(D):
                gather(m, d, 0, V, parts)
                if d < 2:
                    prep_w1(m + 1, 2 * d, 2)
                    for c in (2 * d, 2 * d + 1):
                        for n in range(2):
                            mm1(nxt, c, m + 1, n)
                if d == 1:
                    gelu(m + 1, nxt)
                sums(d, parts[d], 0, V, banks)
            for b in range(4):
                put_zT(m, b, banks)

        w2_grouped = stage.tile([P, N, PACK], BF16, name="w2grouped", bufs=1, align_bytes=64)
        for s in range(2):
            interleave("s", w2_grouped[:, s * 256 : (s + 1) * 256, :], w2_raw[:, :, s * 256 : (s + 1) * 256])

        def turn_back(b, grouped, at, engine):
            back = psum.tile([P, PACK, P], BF16, name="back", tag="back", bufs=2)
            for t in range(PACK):
                nc.tensor.transpose(back[:, t, :], zT[:, b, t, :], ident16[:])
            view = back[:].rearrange("p t v -> p v t")
            if engine == "s":
                nc.scalar.copy(grouped[:, at : at + P, :], view)
            else:
                nc.vector.tensor_copy(grouped[:, at : at + P, :], view)

        def second(grouped, v0, vn, tags):
            cols = slice(v0, v0 + vn)
            quantize(z_codes[:, cols], z_scales[:, cols], grouped)
            for a in range(2):
                o = psum.tile([P, 2, vn], F32, name="o", tag=tags[a])
                for i in range(2):
                    mt = 2 * a + i
                    nc.tensor.matmul_mx(
                        out=o[:, i, :],
                        lhsT=w2_codes[:, mt * P : (mt + 1) * P].bitcast(FP8X4),
                        lhsT_scale=w2_scales[:, mt * P : (mt + 1) * P],
                        rhs=z_codes[:, cols].bitcast(FP8X4),
                        rhs_scale=z_scales[:, cols],
                        start=True,
                        stop=True,
                    )
                res = stage.tile([P, 2, vn], F32, name="res", tag="res", bufs=6, align_bytes=64)
                if a == 0 and v0 == 384:
                    nc.vector.tensor_copy(res[:], o[:])
                else:
                    nc.scalar.copy(res[:], o[:])
                nc.sync.dma_start(
                    out=out[a * 256 : (a + 1) * 256, cols].rearrange("(i p) v -> p i v", p=P), in_=res[:]
                )

        CHUNKS = [(0, 256, ("acc0", "acc1")), (256, 128, ("zs0", "zs1")), (384, 128, ("acc0", "acc1"))]
        for v0, vn, tags in CHUNKS:
            grouped = keep.tile([P, vn, PACK], BF16, name=f"zg{v0}", align_bytes=64)
            blocks = range(v0 // P, (v0 + vn) // P)
            banks = {b: new_bank(b) for b in blocks}
            parts = []
            for d in range(D):
                gather(3, d, v0, vn, parts)
                sums(d, parts[d], v0, vn, banks)
                if v0 == 0 and d == 1:
                    quantize(w2_codes[:], w2_scales[:], w2_grouped)
            for b in blocks:
                put_zT(3, b, banks)
            for b in blocks:
                turn_back(b, grouped, b * P - v0, "v" if b == 3 else "s")
            second(grouped, v0, vn, tags)
